import numpy as np
import ml_dtypes


def mxq(x, axis, fmt="e4m3"):
    dtype, down = {"e4m3": (ml_dtypes.float8_e4m3fn, 7), "e5m2": (ml_dtypes.float8_e5m2, 14)}[fmt]
    v = np.moveaxis(np.asarray(x, np.float32).astype(ml_dtypes.bfloat16).astype(np.float64), axis, -1)
    blocks = v.reshape(v.shape[:-1] + (-1, 32))
    amax = np.abs(blocks).max(-1, keepdims=True)
    byte = np.maximum(np.where(amax > 0, np.frexp(amax)[1] - 1 + 127, 0) - down, 1)
    scale = np.exp2(byte - 127.0)
    codes = (blocks / scale).astype(np.float32).astype(dtype).astype(np.float64)
    return np.moveaxis((codes * scale).reshape(v.shape), -1, axis)


WIDE = False


def mx_kscale(k):
    if not WIDE:
        return np.ones(k)
    levels = np.array([30, -30])
    if k % 512:
        return np.exp2(np.random.permutation(np.resize(levels, k // 32))).repeat(32)
    a = np.empty((k // 512, 16))
    for p in range(k // 512):
        a[p, :8] = np.random.permutation(np.resize(levels, 8))
        for g in range(8):
            far = levels[np.abs(levels - a[p, g]) >= 10]
            a[p, g + 8] = far[np.random.randint(len(far))]
    return np.exp2(a.ravel()).repeat(32)


def f64(x):
    return np.asarray(x).astype(np.float64)


def striped(idx):
    return np.tile(np.asarray(idx).reshape(-1, 16).T, (8, 1)).astype(np.uint16)


def unstriped(offs):
    return offs[:16].T.reshape(-1).astype(np.int64)


E2M1 = np.array([0.0, 0.5, 1.0, 1.5, 2.0, 3.0, 4.0, 6.0, -0.0, -0.5, -1.0, -1.5, -2.0, -3.0, -4.0, -6.0])


def pack_weight(w, fmt):
    k, n = w.shape
    w = f64(np.asarray(w, np.float32).astype(ml_dtypes.bfloat16)).reshape(k // 32, 32, n)
    amax = np.abs(w).max(1)
    if fmt in ("e4m3", "e5m2"):
        byte = np.frexp(amax)[1] - 1 + 127 - (7 if fmt == "e4m3" else 14)
    else:
        mant, ex = np.frexp(amax / 6.0)
        byte = np.where(mant > 0.5, ex, ex - 1) + 127
    byte = np.clip(np.where(amax > 0, byte, 1), 1, 254)
    scaled = (w * np.exp2(127.0 - byte)[:, None, :]).reshape(k, n).astype(np.float32)
    by_word = np.ascontiguousarray(scaled.reshape(k // 512, 128, 4, n).transpose(0, 1, 3, 2))
    if fmt in ("e4m3", "e5m2"):
        words = by_word.astype(ml_dtypes.float8_e4m3fn if fmt == "e4m3" else ml_dtypes.float8_e5m2).view(np.uint8)
    else:
        c = by_word.astype(ml_dtypes.float4_e2m1fn).view(np.uint8) & 0xF
        words = (c[..., 0::2] | (c[..., 1::2] << 4)).reshape(k // 512, 128, 2 * n)
    return np.ascontiguousarray(words), np.ascontiguousarray(byte.astype(np.uint8).reshape(k // 512, 16, n))


def unpack_weight(words, scales, fmt):
    g, _, n = scales.shape
    words = np.ascontiguousarray(words).reshape(g, 128, n, -1)
    if fmt in ("e4m3", "e5m2"):
        vals = words.view(ml_dtypes.float8_e4m3fn if fmt == "e4m3" else ml_dtypes.float8_e5m2).astype(np.float64)
    else:
        nib = np.empty((g, 128, n, 4), np.uint8)
        nib[..., 0::2] = words & 0xF
        nib[..., 1::2] = words >> 4
        vals = E2M1[nib]
    vals = vals * np.repeat(np.exp2(scales.astype(np.float64) - 127.0), 8, axis=1)[..., None]
    return vals.transpose(0, 1, 3, 2).reshape(g * 512, n)


K, F, T, Z, J, R, C, D, N = 512, 512, 1024, 1024, 256, 512, 512, 512, 256


def setup_inputs():
    n = np.random.standard_normal
    idx = np.random.permutation(T)[:J]
    idx2 = np.random.permutation(Z)[:J]
    idx3 = np.random.permutation(C)[:J]
    idx4 = np.random.permutation(D)[:J]
    idx5 = np.random.permutation(C)[:J]
    idx6 = np.random.permutation(D)[:J]
    fk = mx_kscale(K)
    fr = mx_kscale(R)
    ff = mx_kscale(F)
    xtp = pack_weight(n((K, T)) / fk[:, None], "e2m1")
    wp = pack_weight(n((K, R)) * 1 / np.sqrt(K) * fk[:, None] * fr, "e5m2")
    xop = pack_weight(n((F, Z)) / ff[:, None], "e5m2")
    w2p = pack_weight(n((F, R)) * 1 / np.sqrt(F) * ff[:, None] * fr, "e4m3")
    wbp = pack_weight(n((R, N)) * 1 / np.sqrt(R) / fr[:, None], "e4m3")
    return {
        "xt_words": xtp[0],
        "xt_scales": xtp[1],
        "w_words": wp[0],
        "w_scales": wp[1],
        "xo_words": xop[0],
        "xo_scales": xop[1],
        "w2_words": w2p[0],
        "w2_scales": w2p[1],
        "wb_words": wbp[0],
        "wb_scales": wbp[1],
        "offs": striped(idx),
        "offs2": striped(idx2),
        "offs3": striped(idx3),
        "offs4": striped(idx4),
        "offs5": striped(idx5),
        "offs6": striped(idx6),
    }


def reference(xt_words, xt_scales, w_words, w_scales, xo_words, xo_scales, w2_words, w2_scales, wb_words, wb_scales, offs, offs2, offs3, offs4, offs5, offs6):
    idx = unstriped(offs)
    idx2 = unstriped(offs2)
    idx3 = unstriped(offs3)
    idx4 = unstriped(offs4)
    idx5 = unstriped(offs5)
    idx6 = unstriped(offs6)
    xtu = unpack_weight(xt_words, xt_scales, "e2m1")
    wu = unpack_weight(w_words, w_scales, "e5m2")
    xou = unpack_weight(xo_words, xo_scales, "e5m2")
    w2u = unpack_weight(w2_words, w2_scales, "e4m3")
    wbu = unpack_weight(wb_words, wb_scales, "e4m3")
    xtidxg = xtu[:, idx]
    a = wu.T @ xtidxg
    xoidx2g = xou[:, idx2]
    b = w2u.T @ xoidx2g
    pw = np.zeros((R, C))
    pw[:, idx3] = a
    pv = np.zeros((R, D))
    pv[:, idx4] = b
    hid = np.maximum(pw[:, idx5] - b, pv[:, idx6] - a)
    hidq = mxq(hid, 0, "e5m2")
    y = wbu.T @ hidq
    return y

@@ -1,0 +1,185 @@
+from contextlib import ExitStack
+
+import concourse.mybir as mybir
+
+F32 = mybir.dt.float32
+BF16 = mybir.dt.bfloat16
+I32 = mybir.dt.int32
+U32 = mybir.dt.uint32
+U16 = mybir.dt.uint16
+U8 = mybir.dt.uint8
+E2M1X4 = mybir.dt.float4_e2m1fn_x4
+E5M2X4 = mybir.dt.float8_e5m2_x4
+E4M3X4 = mybir.dt.float8_e4m3fn_x4
+COPY = mybir.ActivationFunctionType.Copy
+SUBTRACT = mybir.AluOpType.subtract
+MAX = mybir.AluOpType.max
+
+P = 128
+PACK = 4
+K, T, J, R, C, N = 512, 1024, 256, 512, 512, 256
+FLOPS = 2 * (2 * K * R * J) + 2 * R * N * J
+
+
+def tile_list_crossread_twotab_one_plain_kernel(
+    tc, xt_words, xt_scales, w_words, w_scales, xo_words, xo_scales, w2_words, w2_scales,
+    wb_words, wb_scales, offs, offs2, offs3, offs4, offs5, offs6, out,
+):
+    nc = tc.nc
+    with ExitStack() as ctx:
+        lists = ctx.enter_context(tc.tile_pool(name="lists", bufs=1))
+        sb = ctx.enter_context(tc.tile_pool(name="sb", bufs=1))
+        ps = ctx.enter_context(tc.psum_pool(name="ps", bufs=1))
+
+        def tile(shape, dtype, name):
+            return sb.tile(shape, dtype, name=name, align_bytes=64)
+
+        def load_list(src, name):
+            dst = lists.tile([P, J // 16], U16, name=name)
+            nc.sync.dma_start(dst[:], src)
+            return dst
+
+        def plane(width, name):
+            dst = tile([P, width], U8, name)
+            nc.vector.memset(dst[:].bitcast(I32), 0)
+            return dst
+
+        def load_scale_rows(queue, dst, src, rows):
+            for r in rows:
+                queue.dma_start(dst[:].bitcast(I32)[r:P:32, :], src[0].bitcast(I32)[r:16:4, :])
+
+        def load_words(queue, src, width, name):
+            dst = tile([P, width], U32, name)
+            queue.dma_start(dst[:].bitcast(I32), src[0].rearrange("p n t -> p (n t)").bitcast(I32))
+            return dst
+
+        def deal(words, scales, name):
+            dealt_words = tile([P, R], U32, name + "_words_dealt")
+            nc.vector.tensor_copy(
+                dealt_words[:].bitcast(I32).rearrange("p (t c i) -> p c t i", t=PACK, i=4),
+                words[:].bitcast(I32).rearrange("p (c i t) -> p c t i", t=PACK, i=4),
+            )
+            dealt_scales = tile([P, R], U8, name + "_scales_dealt")
+            nc.vector.tensor_copy(
+                dealt_scales[:].rearrange("p (t m) -> p t m", t=PACK),
+                scales[:].rearrange("p (m t) -> p t m", t=PACK),
+            )
+            return dealt_words, dealt_scales
+
+        xt_plane = plane(T, "xt_plane")
+        w_plane = plane(R, "w_plane")
+        w2_plane = plane(R, "w2_plane")
+        xo_plane = plane(T, "xo_plane")
+        wb_plane = plane(N, "wb_plane")
+
+        list_xt = load_list(offs, "list_xt")
+        xt_table = tile([P, T], U16, "xt_table")
+        nc.sync.dma_start(xt_table[:].bitcast(I32), xt_words[0].bitcast(I32))
+        w_raw = load_words(nc.sync, w_words, R, "w_raw")
+        load_scale_rows(nc.sync, xt_plane, xt_scales, range(4))
+        load_scale_rows(nc.sync, w_plane, w_scales, range(4))
+        list_pw_put = load_list(offs3, "list_pw_put")
+        list_xo = load_list(offs2, "list_xo")
+        xo_table = load_words(nc.sync, xo_words, T, "xo_table")
+        load_scale_rows(nc.sync, xo_plane, xo_scales, range(4))
+        w2_raw = load_words(nc.gpsimd, w2_words, R, "w2_raw")
+        load_scale_rows(nc.gpsimd, w2_plane, w2_scales, range(2))
+        load_scale_rows(nc.sync, w2_plane, w2_scales, range(2, 4))
+        list_pv_put = load_list(offs4, "list_pv_put")
+        list_pw_get = load_list(offs5, "list_pw_get")
+        list_pv_get = load_list(offs6, "list_pv_get")
+        wb_codes = load_words(nc.sync, wb_words, N, "wb_codes")
+        load_scale_rows(nc.sync, wb_plane, wb_scales, range(4))
+
+        pw = [tile([P, C], F32, "pw%d" % t) for t in range(PACK)]
+        pv = [tile([P, C], F32, "pv%d" % t) for t in range(PACK)]
+        for board in pw:
+            nc.vector.memset(board[:], 0.0)
+
+        xt_codes = tile([P, J], U16, "xt_codes")
+        nc.vector.tensor_copy(xt_codes[:], xt_table[:].indirect(list_xt[:]))
+        xt_bytes = tile([P, J], U8, "xt_bytes")
+        nc.vector.tensor_copy(xt_bytes[:], xt_plane[:].indirect(list_xt[:]))
+        w_codes, w_bytes = deal(w_raw, w_plane, "w")
+
+        a_banks = [ps.tile([P, n, J], F32, name="a_bank%d" % i) for i, n in enumerate((1, 1, 2))]
+        a_psum = [a_banks[0][:, 0, :], a_banks[1][:, 0, :], a_banks[2][:, 0, :], a_banks[2][:, 1, :]]
+        for t in range(PACK):
+            cols = slice(t * P, (t + 1) * P)
+            nc.tensor.matmul_mx(
+                out=a_psum[t], lhsT=w_codes[:, cols].bitcast(E5M2X4), lhsT_scale=w_bytes[:, cols],
+                rhs=xt_codes[:].bitcast(E2M1X4), rhs_scale=xt_bytes[:], start=True, stop=True,
+            )
+        a = tile([P, PACK, J], F32, "a")
+        nc.vector.tensor_copy(a[:, 2:4, :], a_banks[2][:])
+        for t in range(PACK):
+            if t < 2:
+                nc.scalar.activation(a[:, t : t + 1, :], a_banks[t][:], COPY)
+            nc.scalar.activation(pw[t][:].indirect(list_pw_put[:]), a[:, t, :], COPY)
+
+        for board in pv:
+            nc.vector.memset(board[:], 0.0)
+
+        xo_codes = tile([P, J], U32, "xo_codes")
+        nc.vector.tensor_copy(xo_codes[:], xo_table[:].indirect(list_xo[:]))
+        xo_bytes = tile([P, J], U8, "xo_bytes")
+        nc.vector.tensor_copy(xo_bytes[:], xo_plane[:].indirect(list_xo[:]))
+        w2_codes, w2_bytes = deal(w2_raw, w2_plane, "w2")
+
+        b_banks = [ps.tile([P, 2, J], F32, name="b_bank%d" % i) for i in range(2)]
+        for t in range(PACK):
+            cols = slice(t * P, (t + 1) * P)
+            nc.tensor.matmul_mx(
+                out=b_banks[t // 2][:, t % 2, :], lhsT=w2_codes[:, cols].bitcast(E4M3X4), lhsT_scale=w2_bytes[:, cols],
+                rhs=xo_codes[:].bitcast(E5M2X4), rhs_scale=xo_bytes[:], start=True, stop=True,
+            )
+        b = tile([P, PACK, J], F32, "b")
+        for h in range(2):
+            nc.vector.tensor_copy(b[:, 2 * h : 2 * h + 2, :], b_banks[h][:])
+        for t in (0, 1):
+            nc.vector.tensor_copy(pv[t][:].indirect(list_pv_put[:]), b[:, t, :])
+        for t in (2, 3):
+            nc.scalar.activation(pv[t][:].indirect(list_pv_put[:]), b[:, t, :], COPY)
+
+        dw = tile([P, PACK, J], F32, "dw")
+        dv = tile([P, PACK, J], F32, "dv")
+
+        def diff_w(t):
+            nc.vector.tensor_tensor(dw[:, t, :], pw[t][:].indirect(list_pw_get[:]), b[:, t, :], SUBTRACT)
+
+        def diff_v(t):
+            nc.vector.tensor_tensor(dv[:, t, :], pv[t][:].indirect(list_pv_get[:]), a[:, t, :], SUBTRACT)
+
+        for t in range(3):
+            diff_w(t)
+        diff_v(0)
+        diff_v(1)
+        diff_w(3)
+        diff_v(2)
+        diff_v(3)
+
+        hid = tile([P, J * PACK], BF16, "hid")
+        nc.vector.tensor_tensor(
+            hid[:].rearrange("p (c i t) -> p c t i", t=PACK, i=4),
+            dw[:].rearrange("p t (c i) -> p c t i", i=4),
+            dv[:].rearrange("p t (c i) -> p c t i", i=4),
+            MAX,
+        )
+        hid_codes = tile([P, J], U32, "hid_codes")
+        hid_bytes = tile([P, J], U8, "hid_bytes")
+        nc.vector.quantize_mx(out=hid_codes[:].bitcast(E5M2X4), scales=hid_bytes[:], in_=hid[:])
+
+        for h in range(2):
+            cols = slice(h * P, (h + 1) * P)
+            y_bank = ps.tile([P, J], F32, name="y_bank%d" % h)
+            nc.tensor.matmul_mx(
+                out=y_bank[:], lhsT=wb_codes[:, cols].bitcast(E4M3X4), lhsT_scale=wb_plane[:, cols],
+                rhs=hid_codes[:].bitcast(E5M2X4), rhs_scale=hid_bytes[:], start=True, stop=True,
+            )
+            y = tile([P, J], F32, "y%d" % h)
+            if h == 0:
+                nc.scalar.activation(y[:], y_bank[:], COPY)
+                nc.scalar.dma_start(out[cols, :], y[:])
+            else:
+                nc.vector.tensor_copy(y[:], y_bank[:])
+                nc.sync.dma_start(out[cols, :], y[:])

@@ -31,100 +31,112 @@ def tile_list_crossread_twotab_one_plain_kernel(
         sb = ctx.enter_context(tc.tile_pool(name="sb", bufs=1))
         ps = ctx.enter_context(tc.psum_pool(name="ps", bufs=1))
 
-        def tile(shape, dtype, name):
-            return sb.tile(shape, dtype, name=name, align_bytes=64)
+        def tile(shape, dtype, name, tag=None):
+            return sb.tile(shape, dtype, name=name, tag=tag or name, align_bytes=64)
 
         def load_list(src, name):
             dst = lists.tile([P, J // 16], U16, name=name)
             nc.sync.dma_start(dst[:], src)
             return dst
 
-        def plane(width, name):
+        def plane(engine, width, name):
             dst = tile([P, width], U8, name)
-            nc.vector.memset(dst[:].bitcast(I32), 0)
+            engine.memset(dst[:].bitcast(I32), 0)
             return dst
 
         def load_scale_rows(queue, dst, src, rows):
             for r in rows:
                 queue.dma_start(dst[:].bitcast(I32)[r:P:32, :], src[0].bitcast(I32)[r:16:4, :])
 
+        def load_scale_quadrants(queue, dst, src, quadrants):
+            width = dst.shape[1] // 4
+            for q in quadrants:
+                rows = src[0].bitcast(I32)[4 * q : 4 * q + 4, :].unsqueeze(0).to_broadcast([8, 4, width])
+                queue.dma_start(dst[:].bitcast(I32)[32 * q : 32 * q + 32, :], rows)
+
         def load_words(queue, src, width, name):
             dst = tile([P, width], U32, name)
             queue.dma_start(dst[:].bitcast(I32), src[0].rearrange("p n t -> p (n t)").bitcast(I32))
             return dst
 
-        def deal(words, scales, name):
-            dealt_words = tile([P, R], U32, name + "_words_dealt")
-            nc.vector.tensor_copy(
-                dealt_words[:].bitcast(I32).rearrange("p (t c i) -> p c t i", t=PACK, i=4),
-                words[:].bitcast(I32).rearrange("p (c i t) -> p c t i", t=PACK, i=4),
+        def deal_words(copy, words, name):
+            dealt = tile([P, R], U32, name)
+            copy(
+                dealt[:].rearrange("p (t c i) -> p c t i", t=PACK, i=4),
+                words[:].rearrange("p (c i t) -> p c t i", t=PACK, i=4),
             )
-            dealt_scales = tile([P, R], U8, name + "_scales_dealt")
-            nc.vector.tensor_copy(
-                dealt_scales[:].rearrange("p (t m) -> p t m", t=PACK),
+            return dealt
+
+        def deal_scales(copy, scales, name):
+            dealt = tile([P, R], U8, name)
+            copy(
+                dealt[:].rearrange("p (t m) -> p t m", t=PACK),
                 scales[:].rearrange("p (m t) -> p t m", t=PACK),
             )
-            return dealt_words, dealt_scales
+            return dealt
 
-        xt_plane = plane(T, "xt_plane")
-        w_plane = plane(R, "w_plane")
-        w2_plane = plane(R, "w2_plane")
-        xo_plane = plane(T, "xo_plane")
-        wb_plane = plane(N, "wb_plane")
+        w_plane = tile([P, R], U8, "w_plane")
+        xt_plane = plane(nc.vector, T, "xt_plane")
+        w2_plane = plane(nc.gpsimd, R, "w2_plane")
+        xo_plane = plane(nc.vector, T, "xo_plane")
+        wb_plane = plane(nc.vector, N, "wb_plane")
 
         list_xt = load_list(offs, "list_xt")
+        load_scale_quadrants(nc.scalar, w_plane, w_scales, range(3))
+        load_scale_quadrants(nc.sync, w_plane, w_scales, range(3, 4))
         xt_table = tile([P, T], U16, "xt_table")
         nc.sync.dma_start(xt_table[:].bitcast(I32), xt_words[0].bitcast(I32))
         w_raw = load_words(nc.sync, w_words, R, "w_raw")
         load_scale_rows(nc.sync, xt_plane, xt_scales, range(4))
-        load_scale_rows(nc.sync, w_plane, w_scales, range(4))
+        xo_table = load_words(nc.sync, xo_words, T, "xo_table")
         list_pw_put = load_list(offs3, "list_pw_put")
         list_xo = load_list(offs2, "list_xo")
-        xo_table = load_words(nc.sync, xo_words, T, "xo_table")
-        load_scale_rows(nc.sync, xo_plane, xo_scales, range(4))
-        w2_raw = load_words(nc.gpsimd, w2_words, R, "w2_raw")
-        load_scale_rows(nc.gpsimd, w2_plane, w2_scales, range(2))
-        load_scale_rows(nc.sync, w2_plane, w2_scales, range(2, 4))
+        load_scale_rows(nc.sync, xo_plane, xo_scales, range(1))
+        w2_raw = load_words(nc.sync, w2_words, R, "w2_raw")
+        load_scale_rows(nc.sync, xo_plane, xo_scales, range(1, 4))
+        load_scale_rows(nc.gpsimd, w2_plane, w2_scales, range(4))
         list_pv_put = load_list(offs4, "list_pv_put")
         list_pw_get = load_list(offs5, "list_pw_get")
         list_pv_get = load_list(offs6, "list_pv_get")
         wb_codes = load_words(nc.sync, wb_words, N, "wb_codes")
         load_scale_rows(nc.sync, wb_plane, wb_scales, range(4))
 
-        pw = [tile([P, C], F32, "pw%d" % t) for t in range(PACK)]
-        pv = [tile([P, C], F32, "pv%d" % t) for t in range(PACK)]
-        for board in pw:
-            nc.vector.memset(board[:], 0.0)
+        def board(engine, name, tag=None):
+            dst = tile([P, C], F32, name, tag)
+            engine.memset(dst[:], 0.0)
+            return dst
+
+        pw = [board(nc.vector, "pw%d" % t) for t in range(PACK)]
 
         xt_codes = tile([P, J], U16, "xt_codes")
         nc.vector.tensor_copy(xt_codes[:], xt_table[:].indirect(list_xt[:]))
+        w_codes = deal_words(nc.scalar.copy, w_raw, "w_words_dealt")
+        w_bytes = deal_scales(nc.vector.tensor_copy, w_plane, "w_scales_dealt")
         xt_bytes = tile([P, J], U8, "xt_bytes")
         nc.vector.tensor_copy(xt_bytes[:], xt_plane[:].indirect(list_xt[:]))
-        w_codes, w_bytes = deal(w_raw, w_plane, "w")
 
         a_banks = [ps.tile([P, n, J], F32, name="a_bank%d" % i) for i, n in enumerate((1, 1, 2))]
-        a_psum = [a_banks[0][:, 0, :], a_banks[1][:, 0, :], a_banks[2][:, 0, :], a_banks[2][:, 1, :]]
-        for t in range(PACK):
+        a_psum = {0: a_banks[0][:, 0, :], 3: a_banks[1][:, 0, :], 1: a_banks[2][:, 0, :], 2: a_banks[2][:, 1, :]}
+        for t in (0, 3, 1, 2):
             cols = slice(t * P, (t + 1) * P)
             nc.tensor.matmul_mx(
                 out=a_psum[t], lhsT=w_codes[:, cols].bitcast(E5M2X4), lhsT_scale=w_bytes[:, cols],
                 rhs=xt_codes[:].bitcast(E2M1X4), rhs_scale=xt_bytes[:], start=True, stop=True,
             )
         a = tile([P, PACK, J], F32, "a")
-        nc.vector.tensor_copy(a[:, 2:4, :], a_banks[2][:])
-        for t in range(PACK):
-            if t < 2:
-                nc.scalar.activation(a[:, t : t + 1, :], a_banks[t][:], COPY)
+        nc.scalar.activation(a[:, 0:1, :], a_banks[0][:], COPY)
+        nc.vector.tensor_copy(a[:, 3:4, :], a_banks[1][:])
+        nc.scalar.activation(a[:, 1:3, :], a_banks[2][:], COPY)
+        for t in range(3):
             nc.scalar.activation(pw[t][:].indirect(list_pw_put[:]), a[:, t, :], COPY)
-
-        for board in pv:
-            nc.vector.memset(board[:], 0.0)
 
         xo_codes = tile([P, J], U32, "xo_codes")
         nc.vector.tensor_copy(xo_codes[:], xo_table[:].indirect(list_xo[:]))
+        w2_codes = deal_words(nc.gpsimd.tensor_copy, w2_raw, "w2_words_dealt")
+        w2_bytes = deal_scales(nc.gpsimd.tensor_copy, w2_plane, "w2_scales_dealt")
         xo_bytes = tile([P, J], U8, "xo_bytes")
         nc.vector.tensor_copy(xo_bytes[:], xo_plane[:].indirect(list_xo[:]))
-        w2_codes, w2_bytes = deal(w2_raw, w2_plane, "w2")
+        nc.vector.tensor_copy(pw[3][:].indirect(list_pw_put[:]), a[:, 3, :])
 
         b_banks = [ps.tile([P, 2, J], F32, name="b_bank%d" % i) for i in range(2)]
         for t in range(PACK):
@@ -133,12 +145,13 @@ def tile_list_crossread_twotab_one_plain_kernel(
                 out=b_banks[t // 2][:, t % 2, :], lhsT=w2_codes[:, cols].bitcast(E4M3X4), lhsT_scale=w2_bytes[:, cols],
                 rhs=xo_codes[:].bitcast(E5M2X4), rhs_scale=xo_bytes[:], start=True, stop=True,
             )
+        spent = ("w2_words_dealt", "w2_scales_dealt", "xo_codes", "xo_bytes")
+        pv = [board(nc.gpsimd, "pv%d" % t, spent[t]) for t in range(PACK)]
         b = tile([P, PACK, J], F32, "b")
-        for h in range(2):
-            nc.vector.tensor_copy(b[:, 2 * h : 2 * h + 2, :], b_banks[h][:])
-        for t in (0, 1):
-            nc.vector.tensor_copy(pv[t][:].indirect(list_pv_put[:]), b[:, t, :])
-        for t in (2, 3):
+        nc.vector.tensor_copy(b[:, 0:2, :], b_banks[0][:])
+        nc.vector.tensor_copy(b[:, 2:4, :], b_banks[1][:])
+        nc.vector.tensor_copy(pv[0][:].indirect(list_pv_put[:]), b[:, 0, :])
+        for t in (1, 2, 3):
             nc.scalar.activation(pv[t][:].indirect(list_pv_put[:]), b[:, t, :], COPY)
 
         dw = tile([P, PACK, J], F32, "dw")
@@ -150,36 +163,38 @@ def tile_list_crossread_twotab_one_plain_kernel(
         def diff_v(t):
             nc.vector.tensor_tensor(dv[:, t, :], pv[t][:].indirect(list_pv_get[:]), a[:, t, :], SUBTRACT)
 
-        for t in range(3):
+        for t in range(PACK):
             diff_w(t)
-        diff_v(0)
-        diff_v(1)
-        diff_w(3)
-        diff_v(2)
-        diff_v(3)
+        for t in range(PACK):
+            diff_v(t)
 
-        hid = tile([P, J * PACK], BF16, "hid")
-        nc.vector.tensor_tensor(
-            hid[:].rearrange("p (c i t) -> p c t i", t=PACK, i=4),
-            dw[:].rearrange("p t (c i) -> p c t i", i=4),
-            dv[:].rearrange("p t (c i) -> p c t i", i=4),
-            MAX,
-        )
-        hid_codes = tile([P, J], U32, "hid_codes")
-        hid_bytes = tile([P, J], U8, "hid_bytes")
-        nc.vector.quantize_mx(out=hid_codes[:].bitcast(E5M2X4), scales=hid_bytes[:], in_=hid[:])
-
+        half = J // 2
+        hid = [tile([P, half * PACK], BF16, "hid%d" % h) for h in range(2)]
         for h in range(2):
-            cols = slice(h * P, (h + 1) * P)
-            y_bank = ps.tile([P, J], F32, name="y_bank%d" % h)
-            nc.tensor.matmul_mx(
-                out=y_bank[:], lhsT=wb_codes[:, cols].bitcast(E4M3X4), lhsT_scale=wb_plane[:, cols],
-                rhs=hid_codes[:].bitcast(E5M2X4), rhs_scale=hid_bytes[:], start=True, stop=True,
+            slots = slice(h * half, (h + 1) * half)
+            nc.vector.tensor_tensor(
+                hid[h][:].rearrange("p (c i t) -> p c t i", t=PACK, i=4),
+                dw[:, :, slots].rearrange("p t (c i) -> p c t i", i=4),
+                dv[:, :, slots].rearrange("p t (c i) -> p c t i", i=4),
+                MAX,
             )
-            y = tile([P, J], F32, "y%d" % h)
+        for h in range(2):
+            slots = slice(h * half, (h + 1) * half)
+            hid_codes = tile([P, half], U32, "hid_codes%d" % h)
+            hid_bytes = tile([P, half], U8, "hid_bytes%d" % h)
+            nc.vector.quantize_mx(out=hid_codes[:].bitcast(E5M2X4), scales=hid_bytes[:], in_=hid[h][:])
+            y_bank = ps.tile([P, 2, half], F32, name="y_bank%d" % h)
+            for u in range(2):
+                cols = slice(u * P, (u + 1) * P)
+                nc.tensor.matmul_mx(
+                    out=y_bank[:, u, :], lhsT=wb_codes[:, cols].bitcast(E4M3X4), lhsT_scale=wb_plane[:, cols],
+                    rhs=hid_codes[:].bitcast(E5M2X4), rhs_scale=hid_bytes[:], start=True, stop=True,
+                )
+            y = tile([P, 2, half], F32, "y%d" % h)
+            dst = out[:, slots].rearrange("(u p) j -> p u j", p=P)
             if h == 0:
                 nc.scalar.activation(y[:], y_bank[:], COPY)
-                nc.scalar.dma_start(out[cols, :], y[:])
+                nc.scalar.dma_start(dst, y[:])
             else:
                 nc.vector.tensor_copy(y[:], y_bank[:])
-                nc.sync.dma_start(out[cols, :], y[:])
+                nc.sync.dma_start(dst, y[:])

@@ -88,13 +88,13 @@ def tile_list_crossread_twotab_one_plain_kernel(
         nc.sync.dma_start(xt_table[:].bitcast(I32), xt_words[0].bitcast(I32))
         w_raw = load_words(nc.sync, w_words, R, "w_raw")
         load_scale_rows(nc.sync, xt_plane, xt_scales, range(4))
-        xo_table = load_words(nc.sync, xo_words, T, "xo_table")
-        list_pw_put = load_list(offs3, "list_pw_put")
-        list_xo = load_list(offs2, "list_xo")
-        load_scale_rows(nc.sync, xo_plane, xo_scales, range(1))
         w2_raw = load_words(nc.sync, w2_words, R, "w2_raw")
-        load_scale_rows(nc.sync, xo_plane, xo_scales, range(1, 4))
-        load_scale_rows(nc.gpsimd, w2_plane, w2_scales, range(4))
+        xo_table = load_words(nc.sync, xo_words, T, "xo_table")
+        list_xo = load_list(offs2, "list_xo")
+        list_pw_put = load_list(offs3, "list_pw_put")
+        load_scale_rows(nc.sync, xo_plane, xo_scales, range(4))
+        load_scale_rows(nc.gpsimd, w2_plane, w2_scales, range(3))
+        load_scale_rows(nc.sync, w2_plane, w2_scales, range(3, 4))
         list_pv_put = load_list(offs4, "list_pv_put")
         list_pw_get = load_list(offs5, "list_pw_get")
         list_pv_get = load_list(offs6, "list_pv_get")
@@ -106,7 +106,7 @@ def tile_list_crossread_twotab_one_plain_kernel(
             engine.memset(dst[:], 0.0)
             return dst
 
-        pw = [board(nc.vector, "pw%d" % t) for t in range(PACK)]
+        pw = [board(nc.vector, "pw%d" % t) for t in range(PACK - 1)]
 
         xt_codes = tile([P, J], U16, "xt_codes")
         nc.vector.tensor_copy(xt_codes[:], xt_table[:].indirect(list_xt[:]))
@@ -114,6 +114,8 @@ def tile_list_crossread_twotab_one_plain_kernel(
         w_bytes = deal_scales(nc.vector.tensor_copy, w_plane, "w_scales_dealt")
         xt_bytes = tile([P, J], U8, "xt_bytes")
         nc.vector.tensor_copy(xt_bytes[:], xt_plane[:].indirect(list_xt[:]))
+
+        w2_codes = deal_words(nc.scalar.copy, w2_raw, "w2_words_dealt")
 
         a_banks = [ps.tile([P, n, J], F32, name="a_bank%d" % i) for i, n in enumerate((1, 1, 2))]
         a_psum = {0: a_banks[0][:, 0, :], 3: a_banks[1][:, 0, :], 1: a_banks[2][:, 0, :], 2: a_banks[2][:, 1, :]}
@@ -132,10 +134,10 @@ def tile_list_crossread_twotab_one_plain_kernel(
 
         xo_codes = tile([P, J], U32, "xo_codes")
         nc.vector.tensor_copy(xo_codes[:], xo_table[:].indirect(list_xo[:]))
-        w2_codes = deal_words(nc.gpsimd.tensor_copy, w2_raw, "w2_words_dealt")
         w2_bytes = deal_scales(nc.gpsimd.tensor_copy, w2_plane, "w2_scales_dealt")
-        xo_bytes = tile([P, J], U8, "xo_bytes")
+        xo_bytes = tile([P, J], U8, "xo_bytes", "xo_table")
         nc.vector.tensor_copy(xo_bytes[:], xo_plane[:].indirect(list_xo[:]))
+        pw.append(board(nc.vector, "pw3", "xo_plane"))
         nc.vector.tensor_copy(pw[3][:].indirect(list_pw_put[:]), a[:, 3, :])
 
         b_banks = [ps.tile([P, 2, J], F32, name="b_bank%d" % i) for i in range(2)]
@@ -145,7 +147,7 @@ def tile_list_crossread_twotab_one_plain_kernel(
                 out=b_banks[t // 2][:, t % 2, :], lhsT=w2_codes[:, cols].bitcast(E4M3X4), lhsT_scale=w2_bytes[:, cols],
                 rhs=xo_codes[:].bitcast(E5M2X4), rhs_scale=xo_bytes[:], start=True, stop=True,
             )
-        spent = ("w2_words_dealt", "w2_scales_dealt", "xo_codes", "xo_bytes")
+        spent = ("w2_words_dealt", "w2_scales_dealt", "xo_codes", "xo_table")
         pv = [board(nc.gpsimd, "pv%d" % t, spent[t]) for t in range(PACK)]
         b = tile([P, PACK, J], F32, "b")
         nc.vector.tensor_copy(b[:, 0:2, :], b_banks[0][:])

@@ -84,9 +84,9 @@ def tile_list_crossread_twotab_one_plain_kernel(
         list_xt = load_list(offs, "list_xt")
         load_scale_quadrants(nc.scalar, w_plane, w_scales, range(3))
         load_scale_quadrants(nc.sync, w_plane, w_scales, range(3, 4))
+        w_raw = load_words(nc.sync, w_words, R, "w_raw")
         xt_table = tile([P, T], U16, "xt_table")
         nc.sync.dma_start(xt_table[:].bitcast(I32), xt_words[0].bitcast(I32))
-        w_raw = load_words(nc.sync, w_words, R, "w_raw")
         load_scale_rows(nc.sync, xt_plane, xt_scales, range(4))
         w2_raw = load_words(nc.sync, w2_words, R, "w2_raw")
         xo_table = load_words(nc.sync, xo_words, T, "xo_table")
@@ -106,7 +106,7 @@ def tile_list_crossread_twotab_one_plain_kernel(
             engine.memset(dst[:], 0.0)
             return dst
 
-        pw = [board(nc.vector, "pw%d" % t) for t in range(PACK - 1)]
+        pw = [board(nc.vector, "pw%d" % t) for t in range(PACK)]
 
         xt_codes = tile([P, J], U16, "xt_codes")
         nc.vector.tensor_copy(xt_codes[:], xt_table[:].indirect(list_xt[:]))
@@ -125,9 +125,8 @@ def tile_list_crossread_twotab_one_plain_kernel(
                 out=a_psum[t], lhsT=w_codes[:, cols].bitcast(E5M2X4), lhsT_scale=w_bytes[:, cols],
                 rhs=xt_codes[:].bitcast(E2M1X4), rhs_scale=xt_bytes[:], start=True, stop=True,
             )
-        a = tile([P, PACK, J], F32, "a")
+        a = tile([P, PACK - 1, J], F32, "a")
         nc.scalar.activation(a[:, 0:1, :], a_banks[0][:], COPY)
-        nc.vector.tensor_copy(a[:, 3:4, :], a_banks[1][:])
         nc.scalar.activation(a[:, 1:3, :], a_banks[2][:], COPY)
         for t in range(3):
             nc.scalar.activation(pw[t][:].indirect(list_pw_put[:]), a[:, t, :], COPY)
@@ -137,21 +136,25 @@ def tile_list_crossread_twotab_one_plain_kernel(
         w2_bytes = deal_scales(nc.gpsimd.tensor_copy, w2_plane, "w2_scales_dealt")
         xo_bytes = tile([P, J], U8, "xo_bytes", "xo_table")
         nc.vector.tensor_copy(xo_bytes[:], xo_plane[:].indirect(list_xo[:]))
-        pw.append(board(nc.vector, "pw3", "xo_plane"))
-        nc.vector.tensor_copy(pw[3][:].indirect(list_pw_put[:]), a[:, 3, :])
+        a_last = tile([P, J], F32, "a_last", "xo_plane")
+        nc.vector.tensor_copy(a_last[:], a_banks[1][:, 0, :])
+        nc.vector.tensor_copy(pw[3][:].indirect(list_pw_put[:]), a_last[:])
+        a_rows = [a[:, 0, :], a[:, 1, :], a[:, 2, :], a_last[:]]
 
-        b_banks = [ps.tile([P, 2, J], F32, name="b_bank%d" % i) for i in range(2)]
+        b_banks = [ps.tile([P, n, J], F32, name="b_bank%d" % i) for i, n in enumerate((2, 1, 1))]
+        b_psum = [b_banks[0][:, 0, :], b_banks[0][:, 1, :], b_banks[1][:, 0, :], b_banks[2][:, 0, :]]
         for t in range(PACK):
             cols = slice(t * P, (t + 1) * P)
             nc.tensor.matmul_mx(
-                out=b_banks[t // 2][:, t % 2, :], lhsT=w2_codes[:, cols].bitcast(E4M3X4), lhsT_scale=w2_bytes[:, cols],
+                out=b_psum[t], lhsT=w2_codes[:, cols].bitcast(E4M3X4), lhsT_scale=w2_bytes[:, cols],
                 rhs=xo_codes[:].bitcast(E5M2X4), rhs_scale=xo_bytes[:], start=True, stop=True,
             )
         spent = ("w2_words_dealt", "w2_scales_dealt", "xo_codes", "xo_table")
         pv = [board(nc.gpsimd, "pv%d" % t, spent[t]) for t in range(PACK)]
         b = tile([P, PACK, J], F32, "b")
         nc.vector.tensor_copy(b[:, 0:2, :], b_banks[0][:])
-        nc.vector.tensor_copy(b[:, 2:4, :], b_banks[1][:])
+        nc.vector.tensor_copy(b[:, 2:3, :], b_banks[1][:])
+        nc.scalar.activation(b[:, 3:4, :], b_banks[2][:], COPY)
         nc.vector.tensor_copy(pv[0][:].indirect(list_pv_put[:]), b[:, 0, :])
         for t in (1, 2, 3):
             nc.scalar.activation(pv[t][:].indirect(list_pv_put[:]), b[:, t, :], COPY)
@@ -162,13 +165,16 @@ def tile_list_crossread_twotab_one_plain_kernel(
         def diff_w(t):
             nc.vector.tensor_tensor(dw[:, t, :], pw[t][:].indirect(list_pw_get[:]), b[:, t, :], SUBTRACT)
 
-        def diff_v(t):
-            nc.vector.tensor_tensor(dv[:, t, :], pv[t][:].indirect(list_pv_get[:]), a[:, t, :], SUBTRACT)
+        def diff_v(t, lo, hi):
+            picked = pv[t][:].indirect(list_pv_get[:, lo // 16 : hi // 16])
+            nc.vector.tensor_tensor(dv[:, t, lo:hi], picked, a_rows[t][:, lo:hi], SUBTRACT)
 
         for t in range(PACK):
             diff_w(t)
-        for t in range(PACK):
-            diff_v(t)
+        for t in range(PACK - 1):
+            diff_v(t, 0, J)
+        diff_v(PACK - 1, 0, J // 2)
+        diff_v(PACK - 1, J // 2, J)
 
         half = J // 2
         hid = [tile([P, half * PACK], BF16, "hid%d" % h) for h in range(2)]

from contextlib import ExitStack

import concourse.mybir as mybir

F32 = mybir.dt.float32
BF16 = mybir.dt.bfloat16
I32 = mybir.dt.int32
U32 = mybir.dt.uint32
U16 = mybir.dt.uint16
U8 = mybir.dt.uint8
E2M1X4 = mybir.dt.float4_e2m1fn_x4
E5M2X4 = mybir.dt.float8_e5m2_x4
E4M3X4 = mybir.dt.float8_e4m3fn_x4
COPY = mybir.ActivationFunctionType.Copy
SUBTRACT = mybir.AluOpType.subtract
MAX = mybir.AluOpType.max

P = 128
PACK = 4
K, T, J, R, C, N = 512, 1024, 256, 512, 512, 256
FLOPS = 2 * (2 * K * R * J) + 2 * R * N * J


def tile_list_crossread_twotab_one_plain_kernel(
    tc, xt_words, xt_scales, w_words, w_scales, xo_words, xo_scales, w2_words, w2_scales,
    wb_words, wb_scales, offs, offs2, offs3, offs4, offs5, offs6, out,
):
    nc = tc.nc
    with ExitStack() as ctx:
        lists = ctx.enter_context(tc.tile_pool(name="lists", bufs=1))
        sb = ctx.enter_context(tc.tile_pool(name="sb", bufs=1))
        ps = ctx.enter_context(tc.psum_pool(name="ps", bufs=1))

        def tile(shape, dtype, name, tag=None):
            return sb.tile(shape, dtype, name=name, tag=tag or name, align_bytes=64)

        def load_list(src, name):
            dst = lists.tile([P, J // 16], U16, name=name)
            nc.sync.dma_start(dst[:], src)
            return dst

        def plane(engine, width, name):
            dst = tile([P, width], U8, name)
            engine.memset(dst[:].bitcast(I32), 0)
            return dst

        def load_scale_rows(queue, dst, src, rows):
            for r in rows:
                queue.dma_start(dst[:].bitcast(I32)[r:P:32, :], src[0].bitcast(I32)[r:16:4, :])

        def load_scale_quadrants(queue, dst, src, quadrants):
            width = dst.shape[1] // 4
            for q in quadrants:
                rows = src[0].bitcast(I32)[4 * q : 4 * q + 4, :].unsqueeze(0).to_broadcast([8, 4, width])
                queue.dma_start(dst[:].bitcast(I32)[32 * q : 32 * q + 32, :], rows)

        def load_words(queue, src, width, name):
            dst = tile([P, width], U32, name)
            queue.dma_start(dst[:].bitcast(I32), src[0].rearrange("p n t -> p (n t)").bitcast(I32))
            return dst

        def deal_words(copy, words, name):
            dealt = tile([P, R], U32, name)
            copy(
                dealt[:].rearrange("p (t c i) -> p c t i", t=PACK, i=4),
                words[:].rearrange("p (c i t) -> p c t i", t=PACK, i=4),
            )
            return dealt

        def deal_scales(copy, scales, name):
            dealt = tile([P, R], U8, name)
            copy(
                dealt[:].rearrange("p (t m) -> p t m", t=PACK),
                scales[:].rearrange("p (m t) -> p t m", t=PACK),
            )
            return dealt

        w_plane = tile([P, R], U8, "w_plane")
        xt_plane = plane(nc.vector, T, "xt_plane")
        w2_plane = plane(nc.gpsimd, R, "w2_plane")
        xo_plane = plane(nc.vector, T, "xo_plane")
        wb_plane = plane(nc.vector, N, "wb_plane")

        list_xt = load_list(offs, "list_xt")
        load_scale_quadrants(nc.scalar, w_plane, w_scales, range(3))
        load_scale_quadrants(nc.sync, w_plane, w_scales, range(3, 4))
        w_raw = load_words(nc.sync, w_words, R, "w_raw")
        xt_table = tile([P, T], U16, "xt_table")
        nc.sync.dma_start(xt_table[:].bitcast(I32), xt_words[0].bitcast(I32))
        load_scale_rows(nc.sync, xt_plane, xt_scales, range(4))
        w2_raw = load_words(nc.sync, w2_words, R, "w2_raw")
        xo_table = load_words(nc.sync, xo_words, T, "xo_table")
        list_xo = load_list(offs2, "list_xo")
        list_pw_put = load_list(offs3, "list_pw_put")
        load_scale_rows(nc.sync, xo_plane, xo_scales, range(4))
        load_scale_rows(nc.gpsimd, w2_plane, w2_scales, range(3))
        load_scale_rows(nc.sync, w2_plane, w2_scales, range(3, 4))
        list_pv_put = load_list(offs4, "list_pv_put")
        list_pw_get = load_list(offs5, "list_pw_get")
        list_pv_get = load_list(offs6, "list_pv_get")
        wb_codes = load_words(nc.sync, wb_words, N, "wb_codes")
        load_scale_rows(nc.sync, wb_plane, wb_scales, range(4))

        def board(engine, name, tag=None):
            dst = tile([P, C], F32, name, tag)
            engine.memset(dst[:], 0.0)
            return dst

        pw = [board(nc.vector, "pw%d" % t) for t in range(PACK)]

        xt_codes = tile([P, J], U16, "xt_codes")
        nc.vector.tensor_copy(xt_codes[:], xt_table[:].indirect(list_xt[:]))
        w_codes = deal_words(nc.scalar.copy, w_raw, "w_words_dealt")
        w_bytes = deal_scales(nc.vector.tensor_copy, w_plane, "w_scales_dealt")
        xt_bytes = tile([P, J], U8, "xt_bytes")
        nc.vector.tensor_copy(xt_bytes[:], xt_plane[:].indirect(list_xt[:]))

        w2_codes = deal_words(nc.scalar.copy, w2_raw, "w2_words_dealt")

        a_banks = [ps.tile([P, n, J], F32, name="a_bank%d" % i) for i, n in enumerate((1, 1, 2))]
        a_psum = {0: a_banks[0][:, 0, :], 3: a_banks[1][:, 0, :], 1: a_banks[2][:, 0, :], 2: a_banks[2][:, 1, :]}
        for t in (0, 3, 1, 2):
            cols = slice(t * P, (t + 1) * P)
            nc.tensor.matmul_mx(
                out=a_psum[t], lhsT=w_codes[:, cols].bitcast(E5M2X4), lhsT_scale=w_bytes[:, cols],
                rhs=xt_codes[:].bitcast(E2M1X4), rhs_scale=xt_bytes[:], start=True, stop=True,
            )
        a = tile([P, PACK - 1, J], F32, "a")
        nc.scalar.activation(a[:, 0:1, :], a_banks[0][:], COPY)
        nc.scalar.activation(a[:, 1:3, :], a_banks[2][:], COPY)
        for t in range(3):
            nc.scalar.activation(pw[t][:].indirect(list_pw_put[:]), a[:, t, :], COPY)

        xo_codes = tile([P, J], U32, "xo_codes")
        nc.vector.tensor_copy(xo_codes[:], xo_table[:].indirect(list_xo[:]))
        w2_bytes = deal_scales(nc.gpsimd.tensor_copy, w2_plane, "w2_scales_dealt")
        xo_bytes = tile([P, J], U8, "xo_bytes", "xo_table")
        nc.vector.tensor_copy(xo_bytes[:], xo_plane[:].indirect(list_xo[:]))
        a_last = tile([P, J], F32, "a_last", "xo_plane")
        nc.vector.tensor_copy(a_last[:], a_banks[1][:, 0, :])
        nc.vector.tensor_copy(pw[3][:].indirect(list_pw_put[:]), a_last[:])
        a_rows = [a[:, 0, :], a[:, 1, :], a[:, 2, :], a_last[:]]

        b_banks = [ps.tile([P, n, J], F32, name="b_bank%d" % i) for i, n in enumerate((2, 1, 1))]
        b_psum = [b_banks[0][:, 0, :], b_banks[0][:, 1, :], b_banks[1][:, 0, :], b_banks[2][:, 0, :]]
        for t in range(PACK):
            cols = slice(t * P, (t + 1) * P)
            nc.tensor.matmul_mx(
                out=b_psum[t], lhsT=w2_codes[:, cols].bitcast(E4M3X4), lhsT_scale=w2_bytes[:, cols],
                rhs=xo_codes[:].bitcast(E5M2X4), rhs_scale=xo_bytes[:], start=True, stop=True,
            )
        spent = ("w2_words_dealt", "w2_scales_dealt", "xo_codes", "xo_table")
        pv = [board(nc.gpsimd, "pv%d" % t, spent[t]) for t in range(PACK)]
        b = tile([P, PACK, J], F32, "b")
        nc.vector.tensor_copy(b[:, 0:2, :], b_banks[0][:])
        nc.vector.tensor_copy(b[:, 2:3, :], b_banks[1][:])
        nc.scalar.activation(b[:, 3:4, :], b_banks[2][:], COPY)
        nc.vector.tensor_copy(pv[0][:].indirect(list_pv_put[:]), b[:, 0, :])
        for t in (1, 2, 3):
            nc.scalar.activation(pv[t][:].indirect(list_pv_put[:]), b[:, t, :], COPY)

        dw = tile([P, PACK, J], F32, "dw")
        dv = tile([P, PACK, J], F32, "dv")

        def diff_w(t):
            nc.vector.tensor_tensor(dw[:, t, :], pw[t][:].indirect(list_pw_get[:]), b[:, t, :], SUBTRACT)

        def diff_v(t, lo, hi):
            picked = pv[t][:].indirect(list_pv_get[:, lo // 16 : hi // 16])
            nc.vector.tensor_tensor(dv[:, t, lo:hi], picked, a_rows[t][:, lo:hi], SUBTRACT)

        for t in range(PACK):
            diff_w(t)
        for t in range(PACK - 1):
            diff_v(t, 0, J)
        diff_v(PACK - 1, 0, J // 2)
        diff_v(PACK - 1, J // 2, J)

        half = J // 2
        hid = [tile([P, half * PACK], BF16, "hid%d" % h) for h in range(2)]
        for h in range(2):
            slots = slice(h * half, (h + 1) * half)
            nc.vector.tensor_tensor(
                hid[h][:].rearrange("p (c i t) -> p c t i", t=PACK, i=4),
                dw[:, :, slots].rearrange("p t (c i) -> p c t i", i=4),
                dv[:, :, slots].rearrange("p t (c i) -> p c t i", i=4),
                MAX,
            )
        for h in range(2):
            slots = slice(h * half, (h + 1) * half)
            hid_codes = tile([P, half], U32, "hid_codes%d" % h)
            hid_bytes = tile([P, half], U8, "hid_bytes%d" % h)
            nc.vector.quantize_mx(out=hid_codes[:].bitcast(E5M2X4), scales=hid_bytes[:], in_=hid[h][:])
            y_bank = ps.tile([P, 2, half], F32, name="y_bank%d" % h)
            for u in range(2):
                cols = slice(u * P, (u + 1) * P)
                nc.tensor.matmul_mx(
                    out=y_bank[:, u, :], lhsT=wb_codes[:, cols].bitcast(E4M3X4), lhsT_scale=wb_plane[:, cols],
                    rhs=hid_codes[:].bitcast(E5M2X4), rhs_scale=hid_bytes[:], start=True, stop=True,
                )
            y = tile([P, 2, half], F32, "y%d" % h)
            dst = out[:, slots].rearrange("(u p) j -> p u j", p=P)
            if h == 0:
                nc.scalar.activation(y[:], y_bank[:], COPY)
                nc.scalar.dma_start(dst, y[:])
            else:
                nc.vector.tensor_copy(y[:], y_bank[:])
                nc.sync.dma_start(dst, y[:])
